import numpy as np
import ml_dtypes


def mxq(x, axis, fmt="e4m3"):
    dtype, down = {"e4m3": (ml_dtypes.float8_e4m3fn, 7), "e5m2": (ml_dtypes.float8_e5m2, 14)}[fmt]
    v = np.moveaxis(np.asarray(x, np.float32).astype(ml_dtypes.bfloat16).astype(np.float64), axis, -1)
    blocks = v.reshape(v.shape[:-1] + (-1, 32))
    amax = np.abs(blocks).max(-1, keepdims=True)
    byte = np.maximum(np.where(amax > 0, np.frexp(amax)[1] - 1 + 127, 0) - down, 1)
    scale = np.exp2(byte - 127.0)
    codes = (blocks / scale).astype(np.float32).astype(dtype).astype(np.float64)
    return np.moveaxis((codes * scale).reshape(v.shape), -1, axis)


WIDE = False


def mx_kscale(k):
    if not WIDE:
        return np.ones(k)
    levels = np.array([10, -10, 5, -5, 0])
    if k % 512:
        return np.exp2(np.random.permutation(np.resize(levels, k // 32))).repeat(32)
    a = np.empty((k // 512, 16))
    for p in range(k // 512):
        a[p, :8] = np.random.permutation(np.resize(levels, 8))
        for g in range(8):
            far = levels[np.abs(levels - a[p, g]) >= 10]
            a[p, g + 8] = far[np.random.randint(len(far))]
    return np.exp2(a.ravel()).repeat(32)


def f64(x):
    return np.asarray(x).astype(np.float64)


def striped(idx):
    return np.tile(idx.reshape(-1, 16).T, (8, 1)).astype(np.uint16)


def unstriped(offs):
    return offs[:16].T.reshape(-1).astype(np.int64)


def pack_weight(w):
    k, n = w.shape
    w = f64(np.asarray(w, np.float32).astype(ml_dtypes.bfloat16)).reshape(k // 32, 32, n)
    amax = np.abs(w).max(1)
    byte = np.clip(np.where(amax > 0, np.frexp(amax)[1] - 1 + 127 - 7, 1), 1, 254)
    scaled = (w * np.exp2(127.0 - byte)[:, None, :]).reshape(k, n).astype(np.float32)
    words = np.ascontiguousarray(scaled.reshape(k // 512, 128, 4, n).transpose(0, 1, 3, 2)).astype(ml_dtypes.float8_e4m3fn).view(np.uint8)
    return words, np.ascontiguousarray(byte.astype(np.uint8).reshape(k // 512, 16, n))


def unpack_weight(words, scales):
    g, p, n, _ = words.shape
    vals = np.ascontiguousarray(words).view(ml_dtypes.float8_e4m3fn).astype(np.float64) * np.repeat(np.exp2(scales.astype(np.float64) - 127.0), 8, axis=1)[..., None]
    return vals.transpose(0, 1, 3, 2).reshape(g * 512, n)


def relu(v):
    return np.maximum(v, 0.0)


K, T, S, H, N, W = 512, 2048, 512, 512, 128, 2048
P = 2 ** 7


def setup_inputs():
    n = np.random.standard_normal
    s = mx_kscale(K)[:, None]
    u = mx_kscale(H)
    packed_xT = pack_weight(n((K, T)) * s)
    packed_eT = pack_weight(n((K, W)) * s)
    return {
        "x_words": packed_xT[0],
        "x_scales": packed_xT[1],
        "e_words": packed_eT[0],
        "e_scales": packed_eT[1],
        "w1": (n((K, H)) / np.sqrt(K) / s).astype(np.float32),
        "w3": (n((K, H)) / np.sqrt(K) / s).astype(np.float32),
        "lam": (-np.random.uniform(0.0, 2.0, (H, 1))).astype(np.float32),
        "unit": (np.random.uniform(0.5, 1.5, (H, 1)) * u[:, None]).astype(np.float32),
        "tl": (np.tile(np.random.uniform(0.05, 1.0, S), (P, 1))).astype(np.float32),
        "tr2": (np.tile(np.random.uniform(0.05, 1.0, S), (P, 1))).astype(np.float32),
        "w2": (n((H, N)) / np.sqrt(H) / u[:, None]).astype(np.float32),
        "offs": striped(np.random.permutation(T)[:S]),
        "rchild": striped(np.random.permutation(W)[:S]),
    }


def reference(x_words, x_scales, e_words, e_scales, w1, w3, lam, unit, tl, tr2, w2, offs, rchild):
    xq = unpack_weight(x_words, x_scales)[:, unstriped(offs)]
    etl = np.exp(f64(lam) * f64(tl)[:1])
    zl = f64(unit) * (((mxq(f64(w1), 0, "e4m3").T @ xq)) * etl)
    w2q = mxq(f64(w2), 0, "e4m3")
    pzl = relu(w2q.T @ mxq(zl, 0, "e4m3")) + 0.01
    e_rchild = unpack_weight(e_words, e_scales)[:, unstriped(rchild)]
    etr2 = np.exp(f64(lam) * f64(tr2)[:1])
    zr = f64(unit) * (((mxq(f64(w3), 0, "e4m3").T @ e_rchild)) * etr2)
    pzr = relu(w2q.T @ mxq(zr, 0, "e4m3")) + 0.01
    return pzl * pzr

@@ -1,0 +1,265 @@
+from contextlib import ExitStack
+
+import concourse.mybir as mybir
+from concourse.masks import make_identity
+
+F32 = mybir.dt.float32
+BF16 = mybir.dt.bfloat16
+I32 = mybir.dt.int32
+U32 = mybir.dt.uint32
+U16 = mybir.dt.uint16
+U8 = mybir.dt.uint8
+FP8X4 = mybir.dt.float8_e4m3fn_x4
+ALU = mybir.AluOpType
+ACT = mybir.ActivationFunctionType
+
+P = 128
+PACK = 4
+K = 512
+T = 2048
+S = 512
+H = 512
+N = 128
+BLK = 128
+NBLK = S // BLK
+HALF = 64
+FLOOR = 0.01
+
+FLOPS = 2 * (2 * K * H * S + 2 * H * N * S)
+
+
+def tile_picked_yphylo_prod_p_kernel(
+    tc, x_words, x_scales, e_words, e_scales, w1, w3, lam, unit, tl, tr2, w2, offs, rchild, out
+):
+    nc = tc.nc
+    with ExitStack() as ctx:
+        keep = ctx.enter_context(tc.tile_pool(name="keep", bufs=1))
+        zpsum = ctx.enter_context(tc.psum_pool(name="zpsum", bufs=4))
+        spsum = ctx.enter_context(tc.psum_pool(name="spsum", bufs=4))
+
+        def sb(name, shape, dtype):
+            return keep.tile(shape, dtype, name=name, align_bytes=64)
+
+        def words_of(table):
+            return table[0].rearrange("p n t -> p (n t)").bitcast(I32)
+
+        def load_scales(queue, win, table, first):
+            for a in range(PACK):
+                queue.dma_start(
+                    out=win[first + a : P : 32, :].bitcast(I32), in_=table[0][a:16:PACK, :].bitcast(I32)
+                )
+
+        def load_half(name, w, h):
+            raw = sb(name, [P, PACK, PACK * HALF], F32)
+            cols = slice(h * PACK * HALF, (h + 1) * PACK * HALF)
+            nc.sync.dma_start(out=raw[:], in_=w.rearrange("(p j) c -> p j c", j=PACK)[:, :, cols])
+            return raw
+
+        offs_t = keep.tile([P, S // 16], U16, name="offs_t")
+        rch_t = keep.tile([P, S // 16], U16, name="rch_t")
+        xw = sb("xw", [P, T], U32)
+        ew = sb("ew", [P, T], U32)
+        xs = sb("xs", [P, T], U8)
+        es = sb("es", [P, T], U8)
+        lam_t = sb("lam_t", [P, PACK], F32)
+        unit_t = sb("unit_t", [P, PACK], F32)
+        tl_t = sb("tl_t", [P, PACK], F32)
+        tr_t = sb("tr_t", [P, PACK], F32)
+        ident = sb("ident", [P, P], F32)
+
+        nc.vector.memset(xs[:].bitcast(I32), 0)
+        nc.gpsimd.memset(es[:].bitcast(I32), 0)
+        make_identity(nc, ident[:])
+        nc.scalar.dma_start(out=tl_t[:], in_=tl[0].rearrange("(p m) -> p m", m=PACK))
+        nc.scalar.dma_start(out=lam_t[:], in_=lam.rearrange("(p t) o -> p (t o)", t=PACK))
+        nc.scalar.dma_start(out=tr_t[:], in_=tr2[0].rearrange("(p m) -> p m", m=PACK))
+        nc.scalar.dma_start(out=unit_t[:], in_=unit.rearrange("(p t) o -> p (t o)", t=PACK))
+        nc.sync.dma_start(offs_t[:], offs)
+        nc.sync.dma_start(rch_t[:], rchild)
+        w1_raw = [load_half("w1_raw%d" % h, w1, h) for h in range(2)]
+        load_scales(nc.sync, xs, x_scales, 0)
+        nc.sync.dma_start(out=xw[:].bitcast(I32), in_=words_of(x_words))
+        load_scales(nc.sync, es, e_scales, 4)
+        w3_raw = [load_half("w3_raw%d" % h, w3, h) for h in range(2)]
+        nc.sync.dma_start(out=ew[:].bitcast(I32), in_=words_of(e_words))
+        w2_raw = sb("w2_raw", [P, PACK, N], F32)
+        nc.sync.dma_start(out=w2_raw[:], in_=w2.rearrange("(p j) m -> p j m", j=PACK))
+
+        def spread(name, col):
+            bank = spsum.tile([P, PACK, P], F32, name=name, tag="s")
+            for m in range(PACK):
+                nc.tensor.transpose(bank[:, m, :], col[:, m : m + 1].to_broadcast([P, P]), ident[:])
+            return bank
+
+        def decay(name, bank):
+            e = [sb("%s%d" % (name, t), [P, S], F32) for t in range(PACK)]
+            for t in range(PACK):
+                nc.scalar.activation(
+                    out=e[t][:].rearrange("p (n m) -> p n m", m=PACK),
+                    in_=bank[:].rearrange("p m n -> p n m"),
+                    func=ACT.Exp,
+                    scale=lam_t[:, t : t + 1],
+                )
+            return e
+
+        def gather(name, win, lst, dtype):
+            g = sb(name, [P, S], dtype)
+            nc.vector.tensor_copy(g[:], win[:].indirect(lst[:]))
+            return g
+
+        def cast_half(name, raw):
+            grp = sb(name, [P, PACK, HALF, PACK], BF16)
+            dst = grp[:].rearrange("p t m j -> p m j t")
+            src = raw[:].rearrange("p j (m t) -> p m j t", t=PACK)
+            nc.vector.tensor_copy(out=dst, in_=src)
+            return grp
+
+        def quant_half(grp, codes, scales, h):
+            for t in range(PACK):
+                cols = slice(h * HALF, (h + 1) * HALF)
+                nc.vector.quantize_mx(
+                    out=codes[:, t, cols].bitcast(FP8X4),
+                    scales=scales[:, t, cols],
+                    in_=grp[:, t].rearrange("p m j -> p (m j)"),
+                )
+
+        def first_product(name, codes, scales, gw, gs, first, b):
+            bank = zpsum.tile([P, PACK, BLK], F32, name=name, tag="z")
+            cols = slice(b * BLK, (b + 1) * BLK)
+            for t in range(PACK):
+                nc.tensor.matmul_mx(
+                    out=bank[:, t, :],
+                    lhsT=codes[:, t, :].bitcast(FP8X4),
+                    lhsT_scale=scales[:, t, :],
+                    rhs=gw[b // 2][:, (b % 2) * BLK : (b % 2 + 1) * BLK].bitcast(FP8X4),
+                    rhs_scale=gs[first:P, cols],
+                    start=True,
+                    stop=True,
+                )
+            return bank
+
+        def scale_z(bank, factor, b, dst):
+            nc.vector.tensor_tensor(
+                out=dst.rearrange("p (c i) t -> p c t i", i=4),
+                in0=bank[:].rearrange("p t (c i) -> p c t i", i=4),
+                in1=factor[:, :, b * BLK : (b + 1) * BLK].rearrange("p t (c i) -> p c t i", i=4),
+                op=ALU.mult,
+            )
+
+        def quant_z(name, zb, width):
+            codes = sb(name + "c", [P, width], U32)
+            scales = sb(name + "s", [P, width], U8)
+            nc.vector.quantize_mx(
+                out=codes[:].bitcast(FP8X4), scales=scales[:], in_=zb[:].rearrange("p n t -> p (n t)")
+            )
+            return codes, scales
+
+        def second_product(dst, codes, scales):
+            nc.tensor.matmul_mx(
+                out=dst,
+                lhsT=w2c[:].bitcast(FP8X4),
+                lhsT_scale=w2s[:],
+                rhs=codes[:].bitcast(FP8X4),
+                rhs_scale=scales[:],
+                start=True,
+                stop=True,
+            )
+
+        def times_unit(name, e):
+            f = sb(name, [P, PACK, S], F32)
+            for t in range(PACK):
+                nc.gpsimd.tensor_scalar(
+                    out=f[:, t, :], in0=e[t][:], scalar1=unit_t[:, t : t + 1], scalar2=0.0, op0=ALU.mult, op1=ALU.add
+                )
+            return f
+
+        def gather_halves(name, win, lst):
+            parts = []
+            for h in range(2):
+                g = sb("%s%d" % (name, h), [P, S // 2], U32)
+                nc.vector.tensor_copy(g[:], win[:].indirect(lst[:, h * (S // 32) : (h + 1) * (S // 32)]))
+                parts.append(g)
+            return parts
+
+        fl = times_unit("fl", decay("el", spread("tl_bank", tl_t)))
+        fr = times_unit("fr", decay("er", spread("tr_bank", tr_t)))
+        w1c = sb("w1c", [P, PACK, P], U32)
+        w1s = sb("w1s", [P, PACK, P], U8)
+        for h in range(2):
+            quant_half(cast_half("w1g%d" % h, w1_raw[h]), w1c, w1s, h)
+        xs_g = gather("xs_g", xs, offs_t, U8)
+        xw_g = gather_halves("xw_g", xw, offs_t)
+        es_g = gather("es_g", es, rch_t, U8)
+
+        w3g = sb("w3g", [P, PACK, P, PACK], BF16)
+        for h in range(2):
+            nc.scalar.copy(
+                out=w3g[:, :, h * HALF : (h + 1) * HALF, :].rearrange("p t m j -> p m j t"),
+                in_=w3_raw[h][:].rearrange("p j (m t) -> p m j t", t=PACK),
+            )
+
+        zl = sb("zl", [P, S, PACK], BF16)
+        for b in range(NBLK):
+            bank = first_product("zl_bank%d" % b, w1c, w1s, xw_g, xs_g, 0, b)
+            scale_z(bank, fl, b, zl[:, b * BLK : (b + 1) * BLK, :])
+
+        w3c = sb("w3c", [P, PACK, P], U32)
+        w3s = sb("w3s", [P, PACK, P], U8)
+        nc.vector.quantize_mx(
+            out=w3c[:].rearrange("p t m -> p (t m)").bitcast(FP8X4),
+            scales=w3s[:].rearrange("p t m -> p (t m)"),
+            in_=w3g[:].rearrange("p t m j -> p (t m j)"),
+        )
+        zlc, zls = quant_z("zlq", zl, S)
+        ew_g = gather_halves("ew_g", ew, rch_t)
+
+        w2g = sb("w2g", [P, N, PACK], BF16)
+        nc.scalar.copy(
+            out=w2g[:].rearrange("p (c i) j -> p c j i", i=4), in_=w2_raw[:].rearrange("p j (c i) -> p c j i", i=4)
+        )
+        w2c = sb("w2c", [P, N], U32)
+        w2s = sb("w2s", [P, N], U8)
+
+        pieces = [(0, 2), (2, 1), (3, 1)]
+        zr = [sb("zr%d" % i, [P, nb * BLK, PACK], BF16) for i, (b0, nb) in enumerate(pieces)]
+
+        def z_right(i, k):
+            b = pieces[i][0] + k
+            bank = first_product("zr_bank%d" % b, w3c, w3s, ew_g, es_g, 4, b)
+            scale_z(bank, fr, b, zr[i][:, k * BLK : (k + 1) * BLK, :])
+
+        def back_right(i):
+            width = pieces[i][1] * BLK
+            codes, scales = quant_z("zrq%d" % i, zr[i], width)
+            bank = spsum.tile([P, width], F32, name="pr_bank%d" % i, tag="s")
+            second_product(bank[:], codes, scales)
+            r = sb("pr%d" % i, [P, width], F32)
+            nc.scalar.activation(out=r[:], in_=bank[:], func=ACT.Relu)
+            return r
+
+        def finish(i, r):
+            b0, nb = pieces[i]
+            cols = slice(b0 * BLK, (b0 + nb) * BLK)
+            o = sb("o%d" % i, [P, nb * BLK], F32)
+            nc.vector.scalar_tensor_tensor(
+                out=o[:], in0=r[:], scalar=FLOOR, in1=pl[:, cols], op0=ALU.add, op1=ALU.mult
+            )
+            nc.sync.dma_start(out=out[:, cols], in_=o[:])
+
+        z_right(0, 0)
+        nc.vector.quantize_mx(out=w2c[:].bitcast(FP8X4), scales=w2s[:], in_=w2g[:].rearrange("p m j -> p (m j)"))
+        pl_bank = spsum.tile([P, S], F32, name="pl_bank", tag="s")
+        second_product(pl_bank[:], zlc, zls)
+        rl = sb("rl", [P, S], F32)
+        nc.scalar.activation(out=rl[:], in_=pl_bank[:], func=ACT.Relu)
+        pl = sb("pl", [P, S], F32)
+        nc.scalar.activation(out=pl[:], in_=rl[:], func=ACT.Copy, bias=FLOOR)
+        z_right(0, 1)
+        z_right(1, 0)
+        r0 = back_right(0)
+        z_right(2, 0)
+        r1 = back_right(1)
+        finish(0, r0)
+        r2 = back_right(2)
+        finish(1, r1)
+        finish(2, r2)

@@ -58,7 +58,7 @@ def tile_picked_yphylo_prod_p_kernel(
         offs_t = keep.tile([P, S // 16], U16, name="offs_t")
         rch_t = keep.tile([P, S // 16], U16, name="rch_t")
         xw = sb("xw", [P, T], U32)
-        ew = sb("ew", [P, T], U32)
+        ew = keep.tile([P, T], U32, name="ew", tag="ew_then_zlq", align_bytes=64)
         xs = sb("xs", [P, T], U8)
         es = sb("es", [P, T], U8)
         lam_t = sb("lam_t", [P, PACK], F32)
@@ -68,12 +68,12 @@ def tile_picked_yphylo_prod_p_kernel(
         ident = sb("ident", [P, P], F32)
 
         nc.vector.memset(xs[:].bitcast(I32), 0)
-        nc.gpsimd.memset(es[:].bitcast(I32), 0)
+        nc.vector.memset(es[:].bitcast(I32), 0)
+        nc.gpsimd.dma_start(out=unit_t[:], in_=unit.rearrange("(p t) o -> p (t o)", t=PACK))
         make_identity(nc, ident[:])
         nc.scalar.dma_start(out=tl_t[:], in_=tl[0].rearrange("(p m) -> p m", m=PACK))
         nc.scalar.dma_start(out=lam_t[:], in_=lam.rearrange("(p t) o -> p (t o)", t=PACK))
         nc.scalar.dma_start(out=tr_t[:], in_=tr2[0].rearrange("(p m) -> p m", m=PACK))
-        nc.scalar.dma_start(out=unit_t[:], in_=unit.rearrange("(p t) o -> p (t o)", t=PACK))
         nc.sync.dma_start(offs_t[:], offs)
         nc.sync.dma_start(rch_t[:], rchild)
         w1_raw = [load_half("w1_raw%d" % h, w1, h) for h in range(2)]
@@ -140,9 +140,9 @@ def tile_picked_yphylo_prod_p_kernel(
 
         def scale_z(bank, factor, b, dst):
             nc.vector.tensor_tensor(
-                out=dst.rearrange("p (c i) t -> p c t i", i=4),
-                in0=bank[:].rearrange("p t (c i) -> p c t i", i=4),
-                in1=factor[:, :, b * BLK : (b + 1) * BLK].rearrange("p t (c i) -> p c t i", i=4),
+                out=dst.rearrange("p (c i) t -> p c t i", i=2),
+                in0=bank[:].rearrange("p t (c i) -> p c t i", i=2),
+                in1=factor[:, :, b * BLK : (b + 1) * BLK].rearrange("p t (c i) -> p c t i", i=2),
                 op=ALU.mult,
             )
 
@@ -159,8 +159,8 @@ def tile_picked_yphylo_prod_p_kernel(
                 out=dst,
                 lhsT=w2c[:].bitcast(FP8X4),
                 lhsT_scale=w2s[:],
-                rhs=codes[:].bitcast(FP8X4),
-                rhs_scale=scales[:],
+                rhs=codes.bitcast(FP8X4),
+                rhs_scale=scales,
                 start=True,
                 stop=True,
             )
@@ -210,12 +210,14 @@ def tile_picked_yphylo_prod_p_kernel(
             scales=w3s[:].rearrange("p t m -> p (t m)"),
             in_=w3g[:].rearrange("p t m j -> p (t m j)"),
         )
-        zlc, zls = quant_z("zlq", zl, S)
         ew_g = gather_halves("ew_g", ew, rch_t)
+        zlc = keep.tile([P, S], U32, name="zlc", tag="ew_then_zlq", align_bytes=64)
+        zls = sb("zls", [P, S], U8)
+        nc.vector.quantize_mx(out=zlc[:].bitcast(FP8X4), scales=zls[:], in_=zl[:].rearrange("p n t -> p (n t)"))
 
         w2g = sb("w2g", [P, N, PACK], BF16)
         nc.scalar.copy(
-            out=w2g[:].rearrange("p (c i) j -> p c j i", i=4), in_=w2_raw[:].rearrange("p j (c i) -> p c j i", i=4)
+            out=w2g[:].rearrange("p (c i) j -> p c j i", i=2), in_=w2_raw[:].rearrange("p j (c i) -> p c j i", i=2)
         )
         w2c = sb("w2c", [P, N], U32)
         w2s = sb("w2s", [P, N], U8)
@@ -232,7 +234,7 @@ def tile_picked_yphylo_prod_p_kernel(
             width = pieces[i][1] * BLK
             codes, scales = quant_z("zrq%d" % i, zr[i], width)
             bank = spsum.tile([P, width], F32, name="pr_bank%d" % i, tag="s")
-            second_product(bank[:], codes, scales)
+            second_product(bank[:], codes[:], scales[:])
             r = sb("pr%d" % i, [P, width], F32)
             nc.scalar.activation(out=r[:], in_=bank[:], func=ACT.Relu)
             return r
@@ -248,18 +250,20 @@ def tile_picked_yphylo_prod_p_kernel(
 
         z_right(0, 0)
         nc.vector.quantize_mx(out=w2c[:].bitcast(FP8X4), scales=w2s[:], in_=w2g[:].rearrange("p m j -> p (m j)"))
-        pl_bank = spsum.tile([P, S], F32, name="pl_bank", tag="s")
-        second_product(pl_bank[:], zlc, zls)
-        rl = sb("rl", [P, S], F32)
-        nc.scalar.activation(out=rl[:], in_=pl_bank[:], func=ACT.Relu)
         pl = sb("pl", [P, S], F32)
-        nc.scalar.activation(out=pl[:], in_=rl[:], func=ACT.Copy, bias=FLOOR)
+        for h in range(2):
+            cols = slice(h * (S // 2), (h + 1) * (S // 2))
+            pl_bank = spsum.tile([P, S // 2], F32, name="pl_bank%d" % h, tag="s")
+            second_product(pl_bank[:], zlc[:, cols], zls[:, cols])
+            rl = sb("rl%d" % h, [P, S // 2], F32)
+            nc.scalar.activation(out=rl[:], in_=pl_bank[:], func=ACT.Relu)
+            nc.scalar.activation(out=pl[:, cols], in_=rl[:], func=ACT.Copy, bias=FLOOR)
         z_right(0, 1)
         z_right(1, 0)
         r0 = back_right(0)
         z_right(2, 0)
         r1 = back_right(1)
-        finish(0, r0)
         r2 = back_right(2)
+        finish(0, r0)
         finish(1, r1)
         finish(2, r2)

@@ -109,8 +109,8 @@ def tile_picked_yphylo_prod_p_kernel(
 
         def cast_half(name, raw):
             grp = sb(name, [P, PACK, HALF, PACK], BF16)
-            dst = grp[:].rearrange("p t m j -> p m j t")
-            src = raw[:].rearrange("p j (m t) -> p m j t", t=PACK)
+            dst = grp[:].rearrange("p t m j -> p m t j")
+            src = raw[:].rearrange("p j (m t) -> p m t j", t=PACK)
             nc.vector.tensor_copy(out=dst, in_=src)
             return grp
 
@@ -181,6 +181,8 @@ def tile_picked_yphylo_prod_p_kernel(
                 parts.append(g)
             return parts
 
+        warm = sb("warm", [P, 1], F32)
+        nc.scalar.activation(out=warm[:], in_=ident[:, 0:1], func=ACT.Exp)
         fl = times_unit("fl", decay("el", spread("tl_bank", tl_t)))
         fr = times_unit("fr", decay("er", spread("tr_bank", tr_t)))
         w1c = sb("w1c", [P, PACK, P], U32)
@@ -193,10 +195,9 @@ def tile_picked_yphylo_prod_p_kernel(
 
         w3g = sb("w3g", [P, PACK, P, PACK], BF16)
         for h in range(2):
-            nc.scalar.copy(
-                out=w3g[:, :, h * HALF : (h + 1) * HALF, :].rearrange("p t m j -> p m j t"),
-                in_=w3_raw[h][:].rearrange("p j (m t) -> p m j t", t=PACK),
-            )
+            dst = w3g[:, :, h * HALF : (h + 1) * HALF, :].rearrange("p t m j -> p m t j")
+            src = w3_raw[h][:].rearrange("p j (m t) -> p m t j", t=PACK)
+            nc.scalar.copy(out=dst, in_=src)
 
         zl = sb("zl", [P, S, PACK], BF16)
         for b in range(NBLK):

from contextlib import ExitStack

import concourse.mybir as mybir
from concourse.masks import make_identity

F32 = mybir.dt.float32
BF16 = mybir.dt.bfloat16
I32 = mybir.dt.int32
U32 = mybir.dt.uint32
U16 = mybir.dt.uint16
U8 = mybir.dt.uint8
FP8X4 = mybir.dt.float8_e4m3fn_x4
ALU = mybir.AluOpType
ACT = mybir.ActivationFunctionType

P = 128
PACK = 4
K = 512
T = 2048
S = 512
H = 512
N = 128
BLK = 128
NBLK = S // BLK
HALF = 64
FLOOR = 0.01

FLOPS = 2 * (2 * K * H * S + 2 * H * N * S)


def tile_picked_yphylo_prod_p_kernel(
    tc, x_words, x_scales, e_words, e_scales, w1, w3, lam, unit, tl, tr2, w2, offs, rchild, out
):
    nc = tc.nc
    with ExitStack() as ctx:
        keep = ctx.enter_context(tc.tile_pool(name="keep", bufs=1))
        zpsum = ctx.enter_context(tc.psum_pool(name="zpsum", bufs=4))
        spsum = ctx.enter_context(tc.psum_pool(name="spsum", bufs=4))

        def sb(name, shape, dtype):
            return keep.tile(shape, dtype, name=name, align_bytes=64)

        def words_of(table):
            return table[0].rearrange("p n t -> p (n t)").bitcast(I32)

        def load_scales(queue, win, table, first):
            for a in range(PACK):
                queue.dma_start(
                    out=win[first + a : P : 32, :].bitcast(I32), in_=table[0][a:16:PACK, :].bitcast(I32)
                )

        def load_half(name, w, h):
            raw = sb(name, [P, PACK, PACK * HALF], F32)
            cols = slice(h * PACK * HALF, (h + 1) * PACK * HALF)
            nc.sync.dma_start(out=raw[:], in_=w.rearrange("(p j) c -> p j c", j=PACK)[:, :, cols])
            return raw

        offs_t = keep.tile([P, S // 16], U16, name="offs_t")
        rch_t = keep.tile([P, S // 16], U16, name="rch_t")
        xw = sb("xw", [P, T], U32)
        ew = keep.tile([P, T], U32, name="ew", tag="ew_then_zlq", align_bytes=64)
        xs = sb("xs", [P, T], U8)
        es = sb("es", [P, T], U8)
        lam_t = sb("lam_t", [P, PACK], F32)
        unit_t = sb("unit_t", [P, PACK], F32)
        tl_t = sb("tl_t", [P, PACK], F32)
        tr_t = sb("tr_t", [P, PACK], F32)
        ident = sb("ident", [P, P], F32)

        nc.vector.memset(xs[:].bitcast(I32), 0)
        nc.vector.memset(es[:].bitcast(I32), 0)
        nc.gpsimd.dma_start(out=unit_t[:], in_=unit.rearrange("(p t) o -> p (t o)", t=PACK))
        make_identity(nc, ident[:])
        nc.scalar.dma_start(out=tl_t[:], in_=tl[0].rearrange("(p m) -> p m", m=PACK))
        nc.scalar.dma_start(out=lam_t[:], in_=lam.rearrange("(p t) o -> p (t o)", t=PACK))
        nc.scalar.dma_start(out=tr_t[:], in_=tr2[0].rearrange("(p m) -> p m", m=PACK))
        nc.sync.dma_start(offs_t[:], offs)
        nc.sync.dma_start(rch_t[:], rchild)
        w1_raw = [load_half("w1_raw%d" % h, w1, h) for h in range(2)]
        load_scales(nc.sync, xs, x_scales, 0)
        nc.sync.dma_start(out=xw[:].bitcast(I32), in_=words_of(x_words))
        load_scales(nc.sync, es, e_scales, 4)
        w3_raw = [load_half("w3_raw%d" % h, w3, h) for h in range(2)]
        nc.sync.dma_start(out=ew[:].bitcast(I32), in_=words_of(e_words))
        w2_raw = sb("w2_raw", [P, PACK, N], F32)
        nc.sync.dma_start(out=w2_raw[:], in_=w2.rearrange("(p j) m -> p j m", j=PACK))

        def spread(name, col):
            bank = spsum.tile([P, PACK, P], F32, name=name, tag="s")
            for m in range(PACK):
                nc.tensor.transpose(bank[:, m, :], col[:, m : m + 1].to_broadcast([P, P]), ident[:])
            return bank

        def decay(name, bank):
            e = [sb("%s%d" % (name, t), [P, S], F32) for t in range(PACK)]
            for t in range(PACK):
                nc.scalar.activation(
                    out=e[t][:].rearrange("p (n m) -> p n m", m=PACK),
                    in_=bank[:].rearrange("p m n -> p n m"),
                    func=ACT.Exp,
                    scale=lam_t[:, t : t + 1],
                )
            return e

        def gather(name, win, lst, dtype):
            g = sb(name, [P, S], dtype)
            nc.vector.tensor_copy(g[:], win[:].indirect(lst[:]))
            return g

        def cast_half(name, raw):
            grp = sb(name, [P, PACK, HALF, PACK], BF16)
            dst = grp[:].rearrange("p t m j -> p m t j")
            src = raw[:].rearrange("p j (m t) -> p m t j", t=PACK)
            nc.vector.tensor_copy(out=dst, in_=src)
            return grp

        def quant_half(grp, codes, scales, h):
            for t in range(PACK):
                cols = slice(h * HALF, (h + 1) * HALF)
                nc.vector.quantize_mx(
                    out=codes[:, t, cols].bitcast(FP8X4),
                    scales=scales[:, t, cols],
                    in_=grp[:, t].rearrange("p m j -> p (m j)"),
                )

        def first_product(name, codes, scales, gw, gs, first, b):
            bank = zpsum.tile([P, PACK, BLK], F32, name=name, tag="z")
            cols = slice(b * BLK, (b + 1) * BLK)
            for t in range(PACK):
                nc.tensor.matmul_mx(
                    out=bank[:, t, :],
                    lhsT=codes[:, t, :].bitcast(FP8X4),
                    lhsT_scale=scales[:, t, :],
                    rhs=gw[b // 2][:, (b % 2) * BLK : (b % 2 + 1) * BLK].bitcast(FP8X4),
                    rhs_scale=gs[first:P, cols],
                    start=True,
                    stop=True,
                )
            return bank

        def scale_z(bank, factor, b, dst):
            nc.vector.tensor_tensor(
                out=dst.rearrange("p (c i) t -> p c t i", i=2),
                in0=bank[:].rearrange("p t (c i) -> p c t i", i=2),
                in1=factor[:, :, b * BLK : (b + 1) * BLK].rearrange("p t (c i) -> p c t i", i=2),
                op=ALU.mult,
            )

        def quant_z(name, zb, width):
            codes = sb(name + "c", [P, width], U32)
            scales = sb(name + "s", [P, width], U8)
            nc.vector.quantize_mx(
                out=codes[:].bitcast(FP8X4), scales=scales[:], in_=zb[:].rearrange("p n t -> p (n t)")
            )
            return codes, scales

        def second_product(dst, codes, scales):
            nc.tensor.matmul_mx(
                out=dst,
                lhsT=w2c[:].bitcast(FP8X4),
                lhsT_scale=w2s[:],
                rhs=codes.bitcast(FP8X4),
                rhs_scale=scales,
                start=True,
                stop=True,
            )

        def times_unit(name, e):
            f = sb(name, [P, PACK, S], F32)
            for t in range(PACK):
                nc.gpsimd.tensor_scalar(
                    out=f[:, t, :], in0=e[t][:], scalar1=unit_t[:, t : t + 1], scalar2=0.0, op0=ALU.mult, op1=ALU.add
                )
            return f

        def gather_halves(name, win, lst):
            parts = []
            for h in range(2):
                g = sb("%s%d" % (name, h), [P, S // 2], U32)
                nc.vector.tensor_copy(g[:], win[:].indirect(lst[:, h * (S // 32) : (h + 1) * (S // 32)]))
                parts.append(g)
            return parts

        warm = sb("warm", [P, 1], F32)
        nc.scalar.activation(out=warm[:], in_=ident[:, 0:1], func=ACT.Exp)
        fl = times_unit("fl", decay("el", spread("tl_bank", tl_t)))
        fr = times_unit("fr", decay("er", spread("tr_bank", tr_t)))
        w1c = sb("w1c", [P, PACK, P], U32)
        w1s = sb("w1s", [P, PACK, P], U8)
        for h in range(2):
            quant_half(cast_half("w1g%d" % h, w1_raw[h]), w1c, w1s, h)
        xs_g = gather("xs_g", xs, offs_t, U8)
        xw_g = gather_halves("xw_g", xw, offs_t)
        es_g = gather("es_g", es, rch_t, U8)

        w3g = sb("w3g", [P, PACK, P, PACK], BF16)
        for h in range(2):
            dst = w3g[:, :, h * HALF : (h + 1) * HALF, :].rearrange("p t m j -> p m t j")
            src = w3_raw[h][:].rearrange("p j (m t) -> p m t j", t=PACK)
            nc.scalar.copy(out=dst, in_=src)

        zl = sb("zl", [P, S, PACK], BF16)
        for b in range(NBLK):
            bank = first_product("zl_bank%d" % b, w1c, w1s, xw_g, xs_g, 0, b)
            scale_z(bank, fl, b, zl[:, b * BLK : (b + 1) * BLK, :])

        w3c = sb("w3c", [P, PACK, P], U32)
        w3s = sb("w3s", [P, PACK, P], U8)
        nc.vector.quantize_mx(
            out=w3c[:].rearrange("p t m -> p (t m)").bitcast(FP8X4),
            scales=w3s[:].rearrange("p t m -> p (t m)"),
            in_=w3g[:].rearrange("p t m j -> p (t m j)"),
        )
        ew_g = gather_halves("ew_g", ew, rch_t)
        zlc = keep.tile([P, S], U32, name="zlc", tag="ew_then_zlq", align_bytes=64)
        zls = sb("zls", [P, S], U8)
        nc.vector.quantize_mx(out=zlc[:].bitcast(FP8X4), scales=zls[:], in_=zl[:].rearrange("p n t -> p (n t)"))

        w2g = sb("w2g", [P, N, PACK], BF16)
        nc.scalar.copy(
            out=w2g[:].rearrange("p (c i) j -> p c j i", i=2), in_=w2_raw[:].rearrange("p j (c i) -> p c j i", i=2)
        )
        w2c = sb("w2c", [P, N], U32)
        w2s = sb("w2s", [P, N], U8)

        pieces = [(0, 2), (2, 1), (3, 1)]
        zr = [sb("zr%d" % i, [P, nb * BLK, PACK], BF16) for i, (b0, nb) in enumerate(pieces)]

        def z_right(i, k):
            b = pieces[i][0] + k
            bank = first_product("zr_bank%d" % b, w3c, w3s, ew_g, es_g, 4, b)
            scale_z(bank, fr, b, zr[i][:, k * BLK : (k + 1) * BLK, :])

        def back_right(i):
            width = pieces[i][1] * BLK
            codes, scales = quant_z("zrq%d" % i, zr[i], width)
            bank = spsum.tile([P, width], F32, name="pr_bank%d" % i, tag="s")
            second_product(bank[:], codes[:], scales[:])
            r = sb("pr%d" % i, [P, width], F32)
            nc.scalar.activation(out=r[:], in_=bank[:], func=ACT.Relu)
            return r

        def finish(i, r):
            b0, nb = pieces[i]
            cols = slice(b0 * BLK, (b0 + nb) * BLK)
            o = sb("o%d" % i, [P, nb * BLK], F32)
            nc.vector.scalar_tensor_tensor(
                out=o[:], in0=r[:], scalar=FLOOR, in1=pl[:, cols], op0=ALU.add, op1=ALU.mult
            )
            nc.sync.dma_start(out=out[:, cols], in_=o[:])

        z_right(0, 0)
        nc.vector.quantize_mx(out=w2c[:].bitcast(FP8X4), scales=w2s[:], in_=w2g[:].rearrange("p m j -> p (m j)"))
        pl = sb("pl", [P, S], F32)
        for h in range(2):
            cols = slice(h * (S // 2), (h + 1) * (S // 2))
            pl_bank = spsum.tile([P, S // 2], F32, name="pl_bank%d" % h, tag="s")
            second_product(pl_bank[:], zlc[:, cols], zls[:, cols])
            rl = sb("rl%d" % h, [P, S // 2], F32)
            nc.scalar.activation(out=rl[:], in_=pl_bank[:], func=ACT.Relu)
            nc.scalar.activation(out=pl[:, cols], in_=rl[:], func=ACT.Copy, bias=FLOOR)
        z_right(0, 1)
        z_right(1, 0)
        r0 = back_right(0)
        z_right(2, 0)
        r1 = back_right(1)
        r2 = back_right(2)
        finish(0, r0)
        finish(1, r1)
        finish(2, r2)
